import numpy as np
import ml_dtypes


def mxq(x, axis, fmt="e4m3"):
    dtype, down = {"e4m3": (ml_dtypes.float8_e4m3fn, 7), "e5m2": (ml_dtypes.float8_e5m2, 14)}[fmt]
    v = np.moveaxis(np.asarray(x, np.float32).astype(ml_dtypes.bfloat16).astype(np.float64), axis, -1)
    blocks = v.reshape(v.shape[:-1] + (-1, 32))
    amax = np.abs(blocks).max(-1, keepdims=True)
    byte = np.maximum(np.where(amax > 0, np.frexp(amax)[1] - 1 + 127, 0) - down, 1)
    scale = np.exp2(byte - 127.0)
    codes = (blocks / scale).astype(np.float32).astype(dtype).astype(np.float64)
    return np.moveaxis((codes * scale).reshape(v.shape), -1, axis)


WIDE = False


def mx_kscale(k):
    if not WIDE:
        return np.ones(k)
    levels = np.array([10, -10, 5, -5, 0])
    if k % 512:
        return np.exp2(np.random.permutation(np.resize(levels, k // 32))).repeat(32)
    a = np.empty((k // 512, 16))
    for p in range(k // 512):
        a[p, :8] = np.random.permutation(np.resize(levels, 8))
        for g in range(8):
            far = levels[np.abs(levels - a[p, g]) >= 10]
            a[p, g + 8] = far[np.random.randint(len(far))]
    return np.exp2(a.ravel()).repeat(32)


def f64(x):
    return np.asarray(x).astype(np.float64)


def striped(idx):
    return np.tile(idx.reshape(-1, 16).T, (8, 1)).astype(np.uint16)


def unstriped(offs):
    return offs[:16].T.reshape(-1).astype(np.int64)


def pack_weight(w):
    k, n = w.shape
    w = f64(np.asarray(w, np.float32).astype(ml_dtypes.bfloat16)).reshape(k // 32, 32, n)
    amax = np.abs(w).max(1)
    byte = np.clip(np.where(amax > 0, np.frexp(amax)[1] - 1 + 127 - 7, 1), 1, 254)
    scaled = (w * np.exp2(127.0 - byte)[:, None, :]).reshape(k, n).astype(np.float32)
    words = np.ascontiguousarray(scaled.reshape(k // 512, 128, 4, n).transpose(0, 1, 3, 2)).astype(ml_dtypes.float8_e4m3fn).view(np.uint8)
    return words, np.ascontiguousarray(byte.astype(np.uint8).reshape(k // 512, 16, n))


def unpack_weight(words, scales):
    g, p, n, _ = words.shape
    vals = np.ascontiguousarray(words).view(ml_dtypes.float8_e4m3fn).astype(np.float64) * np.repeat(np.exp2(scales.astype(np.float64) - 127.0), 8, axis=1)[..., None]
    return vals.transpose(0, 1, 3, 2).reshape(g * 512, n)


K, T, S, D, N = 512, 2048, 512, 8, 128
P = 2 ** 7


def setup_inputs():
    n = np.random.standard_normal
    s = mx_kscale(K)[:, None]
    packed_xT = pack_weight(n((K, T)) * s)
    packed_eT = pack_weight(n((K, T)) * s)
    packed_dT = pack_weight(n((K, T)) * s)
    return {
        "x_words": packed_xT[0],
        "x_scales": packed_xT[1],
        "e_words": packed_eT[0],
        "e_scales": packed_eT[1],
        "d_words": packed_dT[0],
        "d_scales": packed_dT[1],
        "w1": (n((K, N)) / np.sqrt(K) / s).astype(np.float32),
        "w2": (n((K, N)) / np.sqrt(K) / s).astype(np.float32),
        "dist": (np.tile(np.random.uniform(0.5, 2.0, S), (P, 1))).astype(np.float32),
        "use": (np.tile(np.random.uniform(0.5, 1.0, S), (P, 1))).astype(np.float32),
        "offs": striped(np.random.permutation(T)[:S]),
    }


def reference(x_words, x_scales, e_words, e_scales, d_words, d_scales, w1, w2, dist, use, offs):
    xq = unpack_weight(x_words, x_scales)[:, unstriped(offs)]
    f0 = mxq(f64(w1), 0, "e4m3").T @ xq
    e_offs = unpack_weight(e_words, e_scales)[:, unstriped(offs)]
    w2q = mxq(f64(w2), 0, "e4m3")
    c0 = w2q.T @ e_offs
    d_offs = unpack_weight(d_words, d_scales)[:, unstriped(offs)]
    c1 = w2q.T @ d_offs
    cost = ((np.abs(f0 - c0) + 0.3) * (np.abs(c1 - c0) + 0.3)) * f64(dist)[:1]
    iw = f64(use)[:1] / cost
    wf = iw * (f0 + c1 - c0)
    sw = iw.reshape(len(iw), -1, D).sum(axis=2)
    return (wf.reshape(len(wf), -1, D).sum(axis=2)) / sw

@@ -1,0 +1,178 @@
+from contextlib import ExitStack
+
+import concourse.mybir as mybir
+from concourse.masks import make_identity
+
+K, T, S, D, N = 512, 2048, 512, 8, 128
+P = 128
+PACK = 4
+HALVES = 2
+HALF = S // HALVES
+GROUPS = HALF // D
+OFFSET = 0.3
+FLOPS = 3 * 2 * K * N * S
+
+F32 = mybir.dt.float32
+BF16 = mybir.dt.bfloat16
+I32 = mybir.dt.int32
+U32 = mybir.dt.uint32
+U16 = mybir.dt.uint16
+U8 = mybir.dt.uint8
+FP8X4 = mybir.dt.float8_e4m3fn_x4
+ALU = mybir.AluOpType
+ACT = mybir.ActivationFunctionType
+AX = mybir.AxisListType
+
+
+def tile_picked_ystarfm_pred_p_kernel(
+    tc, x_words, x_scales, e_words, e_scales, d_words, d_scales, w1, w2, dist, use, offs, out
+):
+    nc = tc.nc
+    with ExitStack() as ctx:
+        sb = ctx.enter_context(tc.tile_pool(name="sb", bufs=1))
+        ps = ctx.enter_context(tc.psum_pool(name="ps", bufs=1))
+
+        offsets = sb.tile([P, S // 16], U16, name="offsets")
+        nc.sync.dma_start(offsets[:], offs)
+
+        w_raw = sb.tile([P, 2, PACK, N], F32, name="w_raw")
+        nc.scalar.dma_start(out=w_raw[:, 1, :, :], in_=w2.rearrange("(p j) n -> p j n", j=PACK))
+        nc.scalar.dma_start(out=w_raw[:, 0, :, :], in_=w1.rearrange("(p j) n -> p j n", j=PACK))
+
+        tables = (("e", e_words, e_scales, 0), ("x", x_words, x_scales, 4), ("d", d_words, d_scales, 8))
+        words, planes = {}, {}
+        for name, w_hbm, s_hbm, row0 in tables:
+            words[name] = sb.tile([P, T], U32, name=name + "_words_sb")
+            nc.gpsimd.dma_start(
+                out=words[name][:].bitcast(I32),
+                in_=w_hbm[0].rearrange("p n t -> p (n t)").bitcast(I32),
+            )
+        for name, w_hbm, s_hbm, row0 in tables:
+            planes[name] = sb.tile([P, T + 4], U8, name=name + "_scales_sb")
+            nc.vector.memset(planes[name][:].bitcast(I32), 0)
+            for q in range(4):
+                nc.sync.dma_start(
+                    out=planes[name][32 * q + row0 : 32 * q + row0 + 4, 0:T].bitcast(I32),
+                    in_=s_hbm[0, 4 * q : 4 * q + 4, :].bitcast(I32),
+                )
+
+        warm_in = sb.tile([P, 1], F32, name="warm_in")
+        warm_out = sb.tile([P, 1], F32, name="warm_out")
+        nc.vector.memset(warm_in[:], 1.0)
+        nc.scalar.activation(warm_out[:], warm_in[:], ACT.Abs_reciprocal_sqrt)
+
+        dist4 = sb.tile([P, PACK], F32, name="dist4")
+        use4 = sb.tile([P, PACK], F32, name="use4")
+        nc.gpsimd.dma_start(out=dist4[:], in_=dist[0].rearrange("(p t) -> p t", t=PACK))
+        nc.gpsimd.dma_start(out=use4[:], in_=use[0].rearrange("(p t) -> p t", t=PACK))
+        ident = sb.tile([P, P], F32, name="ident")
+        make_identity(nc, ident[:])
+
+        picked_words, picked_planes = {}, {}
+        for name, w_hbm, s_hbm, row0 in tables:
+            picked_words[name] = sb.tile([P, S], U32, name=name + "_picked_words", align_bytes=64)
+            picked_planes[name] = sb.tile([P, S], U8, name=name + "_picked_scales", align_bytes=64)
+
+        def gather_scales(name):
+            nc.vector.tensor_copy(picked_planes[name][:], planes[name][:, 0:T].indirect(offsets[:]))
+
+        def gather_words(name, lo, hi):
+            nc.vector.tensor_copy(
+                picked_words[name][:, lo:hi], words[name][:].indirect(offsets[:, lo // 16 : hi // 16])
+            )
+
+        gather_scales("e")
+
+        w_bf = sb.tile([P, 2, N, PACK], BF16, name="w_bf", align_bytes=64)
+        nc.scalar.copy(out=w_bf[:], in_=w_raw[:].rearrange("p w j n -> p w n j"))
+        w_codes = sb.tile([P, 2 * N], U32, name="w_codes", align_bytes=64)
+        w_scales = sb.tile([P, 2 * N], U8, name="w_scales", align_bytes=64)
+        nc.vector.quantize_mx(
+            out=w_codes[:].bitcast(FP8X4), scales=w_scales[:], in_=w_bf[:].rearrange("p w n j -> p (w n j)")
+        )
+
+        def product(bank, weight, name, row0, lo, hi):
+            cols = slice(weight * N, (weight + 1) * N)
+            nc.tensor.matmul_mx(
+                out=bank,
+                lhsT=w_codes[:, cols].bitcast(FP8X4),
+                lhsT_scale=w_scales[:, cols],
+                rhs=picked_words[name][:, lo:hi].bitcast(FP8X4),
+                rhs_scale=picked_planes[name][row0:P, lo:hi],
+                start=True,
+                stop=True,
+            )
+
+        def inverse_of_abs_plus_offset(tag, src, width):
+            mag = sb.tile([P, width], F32, name=tag + "_mag")
+            root = sb.tile([P, width], F32, name=tag + "_root")
+            inv = sb.tile([P, width], F32, name=tag + "_inv")
+            nc.scalar.activation(mag[:], src, ACT.Abs)
+            nc.scalar.activation(root[:], mag[:], ACT.Abs_reciprocal_sqrt, bias=OFFSET)
+            nc.scalar.activation(inv[:], root[:], ACT.Square)
+            return inv
+
+        gather_scales("x")
+        gather_words("e", 0, S)
+        c0_ps = ps.tile([P, S], F32, name="c0_ps")
+        product(c0_ps[:], 1, "e", 0, 0, S)
+        c0 = sb.tile([P, S], F32, name="c0")
+        nc.scalar.copy(out=c0[:], in_=c0_ps[:])
+
+        gather_scales("d")
+
+        inv_dist4 = sb.tile([P, PACK], F32, name="inv_dist4")
+        gain4 = sb.tile([P, PACK], F32, name="gain4")
+        nc.vector.reciprocal(inv_dist4[:], dist4[:])
+        nc.vector.tensor_tensor(gain4[:], inv_dist4[:], use4[:], ALU.mult)
+        gain_ps = ps.tile([P, PACK, P], F32, name="gain_ps")
+        for t in range(PACK):
+            nc.tensor.transpose(gain_ps[:, t, :], gain4[:, t : t + 1].to_broadcast([P, P]), ident[:])
+
+        gather_words("x", 0, S)
+        f0_ps = ps.tile([P, S], F32, name="f0_ps")
+        product(f0_ps[:], 0, "x", 4, 0, S)
+        spec = sb.tile([P, S], F32, name="spec")
+        nc.vector.tensor_tensor(spec[:], f0_ps[:], c0[:], ALU.subtract)
+        inv_spec = inverse_of_abs_plus_offset("spec", spec[:], S)
+
+        c1_ps = []
+        for h in range(HALVES):
+            gather_words("d", h * HALF, (h + 1) * HALF)
+            c1_ps.append(ps.tile([P, HALF], F32, name="c1_ps%d" % h))
+            product(c1_ps[h][:], 1, "d", 8, h * HALF, (h + 1) * HALF)
+
+        prior = sb.tile([P, S], F32, name="prior")
+        nc.vector.tensor_tensor(
+            prior[:].rearrange("p (n t) -> p n t", t=PACK),
+            inv_spec[:].rearrange("p (n t) -> p n t", t=PACK),
+            gain_ps[:].rearrange("p t n -> p n t"),
+            ALU.mult,
+        )
+
+        inv_time, moved = [], []
+        for h in range(HALVES):
+            cols = slice(h * HALF, (h + 1) * HALF)
+            change = sb.tile([P, HALF], F32, name="change%d" % h)
+            nc.vector.tensor_tensor(change[:], c1_ps[h][:], c0[:, cols], ALU.subtract)
+            inv_time.append(inverse_of_abs_plus_offset("time%d" % h, change[:], HALF))
+            moved.append(sb.tile([P, HALF], F32, name="moved%d" % h))
+            nc.vector.tensor_tensor(moved[h][:], c1_ps[h][:], spec[:, cols], ALU.add)
+
+        result = sb.tile([P, S // D], F32, name="result")
+        for h in range(HALVES):
+            cols = slice(h * HALF, (h + 1) * HALF)
+            terms = sb.tile([P, 2, HALF], F32, name="terms%d" % h)
+            nc.vector.tensor_tensor(terms[:, 0, :], inv_time[h][:], prior[:, cols], ALU.mult)
+            nc.vector.tensor_tensor(terms[:, 1, :], terms[:, 0, :], moved[h][:], ALU.mult)
+            sums = sb.tile([P, 2, GROUPS], F32, name="sums%d" % h)
+            nc.vector.tensor_reduce(
+                sums[:].rearrange("p q v -> p (q v)"),
+                terms[:].rearrange("p q (v d) -> p (q v) d", d=D),
+                AX.X,
+                ALU.add,
+            )
+            inv_sum = sb.tile([P, GROUPS], F32, name="inv_sum%d" % h)
+            nc.vector.reciprocal(inv_sum[:], sums[:, 0, :])
+            nc.vector.tensor_tensor(result[:, h * GROUPS : (h + 1) * GROUPS], sums[:, 1, :], inv_sum[:], ALU.mult)
+        nc.sync.dma_start(out=out, in_=result[:])

@@ -35,31 +35,28 @@ def tile_picked_ystarfm_pred_p_kernel(
         offsets = sb.tile([P, S // 16], U16, name="offsets")
         nc.sync.dma_start(offsets[:], offs)
 
-        w_raw = sb.tile([P, 2, PACK, N], F32, name="w_raw")
+        w_raw = sb.tile([P, 2, PACK, N], F32, name="w_raw", tag="slot_d", align_bytes=64)
         nc.scalar.dma_start(out=w_raw[:, 1, :, :], in_=w2.rearrange("(p j) n -> p j n", j=PACK))
         nc.scalar.dma_start(out=w_raw[:, 0, :, :], in_=w1.rearrange("(p j) n -> p j n", j=PACK))
 
         tables = (("e", e_words, e_scales, 0), ("x", x_words, x_scales, 4), ("d", d_words, d_scales, 8))
         words, planes = {}, {}
-        for name, w_hbm, s_hbm, row0 in tables:
-            words[name] = sb.tile([P, T], U32, name=name + "_words_sb")
-            nc.gpsimd.dma_start(
-                out=words[name][:].bitcast(I32),
-                in_=w_hbm[0].rearrange("p n t -> p (n t)").bitcast(I32),
-            )
-        for name, w_hbm, s_hbm, row0 in tables:
-            planes[name] = sb.tile([P, T + 4], U8, name=name + "_scales_sb")
+
+        def load_scales(name, s_hbm, row0, tag):
+            planes[name] = sb.tile([P, T], U8, name=name + "_scales_sb", tag=tag)
             nc.vector.memset(planes[name][:].bitcast(I32), 0)
             for q in range(4):
                 nc.sync.dma_start(
-                    out=planes[name][32 * q + row0 : 32 * q + row0 + 4, 0:T].bitcast(I32),
+                    out=planes[name][32 * q + row0 : 32 * q + row0 + 4, :].bitcast(I32),
                     in_=s_hbm[0, 4 * q : 4 * q + 4, :].bitcast(I32),
                 )
 
-        warm_in = sb.tile([P, 1], F32, name="warm_in")
-        warm_out = sb.tile([P, 1], F32, name="warm_out")
-        nc.vector.memset(warm_in[:], 1.0)
-        nc.scalar.activation(warm_out[:], warm_in[:], ACT.Abs_reciprocal_sqrt)
+        def load_words(name, w_hbm, tag):
+            words[name] = sb.tile([P, T], U32, name=name + "_words_sb", tag=tag, align_bytes=64)
+            nc.sync.dma_start(
+                out=words[name][:].bitcast(I32),
+                in_=w_hbm[0].rearrange("p n t -> p (n t)").bitcast(I32),
+            )
 
         dist4 = sb.tile([P, PACK], F32, name="dist4")
         use4 = sb.tile([P, PACK], F32, name="use4")
@@ -68,23 +65,45 @@ def tile_picked_ystarfm_pred_p_kernel(
         ident = sb.tile([P, P], F32, name="ident")
         make_identity(nc, ident[:])
 
+        minus_one = sb.tile([P, PACK], F32, name="minus_one")
+        inv_dist4 = sb.tile([P, PACK], F32, name="inv_dist4")
+        gain4 = sb.tile([P, PACK], F32, name="gain4")
+        nc.gpsimd.memset(minus_one[:], -1.0)
+        nc.gpsimd.tensor_tensor(inv_dist4[:], dist4[:], minus_one[:], ALU.pow)
+        nc.gpsimd.tensor_tensor(gain4[:], inv_dist4[:], use4[:], ALU.mult)
+
+        warm_in = sb.tile([P, 1], F32, name="warm_in", tag="slot_x", align_bytes=64)
+        warm_out = sb.tile([P, 1], F32, name="warm_out", tag="slot_scales_d")
+        nc.vector.memset(warm_in[:], 1.0)
+        nc.scalar.activation(warm_out[:], warm_in[:], ACT.Abs_reciprocal_sqrt)
+        ones = sb.tile([P, 1], F32, name="ones", tag="slot_e", align_bytes=64)
+        offset = sb.tile([P, 1], F32, name="offset")
+        nc.vector.memset(ones[:], 1.0)
+        load_scales("e", e_scales, 0, "scales_e")
+        nc.vector.tensor_single_scalar(offset[:], ones[:], OFFSET, ALU.mult)
+        load_words("e", e_words, "slot_e")
+        load_scales("x", x_scales, 4, "scales_x")
+        load_words("x", x_words, "slot_x")
+        load_scales("d", d_scales, 8, "slot_scales_d")
+
         picked_words, picked_planes = {}, {}
         for name, w_hbm, s_hbm, row0 in tables:
             picked_words[name] = sb.tile([P, S], U32, name=name + "_picked_words", align_bytes=64)
-            picked_planes[name] = sb.tile([P, S], U8, name=name + "_picked_scales", align_bytes=64)
 
-        def gather_scales(name):
-            nc.vector.tensor_copy(picked_planes[name][:], planes[name][:, 0:T].indirect(offsets[:]))
+        def gather_scales(name, tag):
+            picked_planes[name] = sb.tile([P, S], U8, name=name + "_picked_scales", tag=tag, align_bytes=64)
+            nc.vector.tensor_copy(picked_planes[name][:], planes[name][:].indirect(offsets[:]))
 
         def gather_words(name, lo, hi):
             nc.vector.tensor_copy(
                 picked_words[name][:, lo:hi], words[name][:].indirect(offsets[:, lo // 16 : hi // 16])
             )
 
-        gather_scales("e")
+        gather_scales("e", "picked_scales_e")
 
         w_bf = sb.tile([P, 2, N, PACK], BF16, name="w_bf", align_bytes=64)
         nc.scalar.copy(out=w_bf[:], in_=w_raw[:].rearrange("p w j n -> p w n j"))
+        load_words("d", d_words, "slot_d")
         w_codes = sb.tile([P, 2 * N], U32, name="w_codes", align_bytes=64)
         w_scales = sb.tile([P, 2 * N], U8, name="w_scales", align_bytes=64)
         nc.vector.quantize_mx(
@@ -108,31 +127,26 @@ def tile_picked_ystarfm_pred_p_kernel(
             root = sb.tile([P, width], F32, name=tag + "_root")
             inv = sb.tile([P, width], F32, name=tag + "_inv")
             nc.scalar.activation(mag[:], src, ACT.Abs)
-            nc.scalar.activation(root[:], mag[:], ACT.Abs_reciprocal_sqrt, bias=OFFSET)
+            nc.scalar.activation(root[:], mag[:], ACT.Abs_reciprocal_sqrt, bias=offset[:])
             nc.scalar.activation(inv[:], root[:], ACT.Square)
             return inv
 
-        gather_scales("x")
         gather_words("e", 0, S)
-        c0_ps = ps.tile([P, S], F32, name="c0_ps")
+        gather_scales("x", "slot_e")
+        c0_ps = ps.tile([P, S], F32, name="c0_ps", tag="bank_c0")
         product(c0_ps[:], 1, "e", 0, 0, S)
-        c0 = sb.tile([P, S], F32, name="c0")
+        c0 = sb.tile([P, S], F32, name="c0", tag="slot_c0")
         nc.scalar.copy(out=c0[:], in_=c0_ps[:])
 
-        gather_scales("d")
-
-        inv_dist4 = sb.tile([P, PACK], F32, name="inv_dist4")
-        gain4 = sb.tile([P, PACK], F32, name="gain4")
-        nc.vector.reciprocal(inv_dist4[:], dist4[:])
-        nc.vector.tensor_tensor(gain4[:], inv_dist4[:], use4[:], ALU.mult)
-        gain_ps = ps.tile([P, PACK, P], F32, name="gain_ps")
+        gain_ps = ps.tile([P, PACK, P], F32, name="gain_ps", tag="bank_c0")
         for t in range(PACK):
             nc.tensor.transpose(gain_ps[:, t, :], gain4[:, t : t + 1].to_broadcast([P, P]), ident[:])
 
         gather_words("x", 0, S)
+        gather_scales("d", "slot_x")
         f0_ps = ps.tile([P, S], F32, name="f0_ps")
         product(f0_ps[:], 0, "x", 4, 0, S)
-        spec = sb.tile([P, S], F32, name="spec")
+        spec = sb.tile([P, S], F32, name="spec", tag="slot_scales_d")
         nc.vector.tensor_tensor(spec[:], f0_ps[:], c0[:], ALU.subtract)
         inv_spec = inverse_of_abs_plus_offset("spec", spec[:], S)
 
@@ -141,14 +155,6 @@ def tile_picked_ystarfm_pred_p_kernel(
             gather_words("d", h * HALF, (h + 1) * HALF)
             c1_ps.append(ps.tile([P, HALF], F32, name="c1_ps%d" % h))
             product(c1_ps[h][:], 1, "d", 8, h * HALF, (h + 1) * HALF)
-
-        prior = sb.tile([P, S], F32, name="prior")
-        nc.vector.tensor_tensor(
-            prior[:].rearrange("p (n t) -> p n t", t=PACK),
-            inv_spec[:].rearrange("p (n t) -> p n t", t=PACK),
-            gain_ps[:].rearrange("p t n -> p n t"),
-            ALU.mult,
-        )
 
         inv_time, moved = [], []
         for h in range(HALVES):
@@ -159,20 +165,28 @@ def tile_picked_ystarfm_pred_p_kernel(
             moved.append(sb.tile([P, HALF], F32, name="moved%d" % h))
             nc.vector.tensor_tensor(moved[h][:], c1_ps[h][:], spec[:, cols], ALU.add)
 
-        result = sb.tile([P, S // D], F32, name="result")
+        prior = sb.tile([P, S], F32, name="prior", tag="slot_c0")
+        nc.vector.tensor_tensor(
+            prior[:].rearrange("p (n t) -> p n t", t=PACK),
+            inv_spec[:].rearrange("p (n t) -> p n t", t=PACK),
+            gain_ps[:].rearrange("p t n -> p n t"),
+            ALU.mult,
+        )
+
+        sums = sb.tile([P, 2, S // D], F32, name="sums")
         for h in range(HALVES):
             cols = slice(h * HALF, (h + 1) * HALF)
             terms = sb.tile([P, 2, HALF], F32, name="terms%d" % h)
             nc.vector.tensor_tensor(terms[:, 0, :], inv_time[h][:], prior[:, cols], ALU.mult)
             nc.vector.tensor_tensor(terms[:, 1, :], terms[:, 0, :], moved[h][:], ALU.mult)
-            sums = sb.tile([P, 2, GROUPS], F32, name="sums%d" % h)
             nc.vector.tensor_reduce(
-                sums[:].rearrange("p q v -> p (q v)"),
-                terms[:].rearrange("p q (v d) -> p (q v) d", d=D),
+                sums[:, :, h * GROUPS : (h + 1) * GROUPS],
+                terms[:].rearrange("p q (v d) -> p q v d", d=D),
                 AX.X,
                 ALU.add,
             )
-            inv_sum = sb.tile([P, GROUPS], F32, name="inv_sum%d" % h)
-            nc.vector.reciprocal(inv_sum[:], sums[:, 0, :])
-            nc.vector.tensor_tensor(result[:, h * GROUPS : (h + 1) * GROUPS], sums[:, 1, :], inv_sum[:], ALU.mult)
+        inv_sum = sb.tile([P, S // D], F32, name="inv_sum")
+        result = sb.tile([P, S // D], F32, name="result")
+        nc.vector.reciprocal(inv_sum[:], sums[:, 0, :])
+        nc.vector.tensor_tensor(result[:], sums[:, 1, :], inv_sum[:], ALU.mult)
         nc.sync.dma_start(out=out, in_=result[:])

@@ -10,6 +10,7 @@ HALVES = 2
 HALF = S // HALVES
 GROUPS = HALF // D
 OFFSET = 0.3
+W2, W2_NEG, W1 = 0, 1, 2
 FLOPS = 3 * 2 * K * N * S
 
 F32 = mybir.dt.float32
@@ -72,6 +73,7 @@ def tile_picked_ystarfm_pred_p_kernel(
         nc.gpsimd.tensor_tensor(inv_dist4[:], dist4[:], minus_one[:], ALU.pow)
         nc.gpsimd.tensor_tensor(gain4[:], inv_dist4[:], use4[:], ALU.mult)
 
+        load_scales("e", e_scales, 0, "scales_e")
         warm_in = sb.tile([P, 1], F32, name="warm_in", tag="slot_x", align_bytes=64)
         warm_out = sb.tile([P, 1], F32, name="warm_out", tag="slot_scales_d")
         nc.vector.memset(warm_in[:], 1.0)
@@ -79,7 +81,6 @@ def tile_picked_ystarfm_pred_p_kernel(
         ones = sb.tile([P, 1], F32, name="ones", tag="slot_e", align_bytes=64)
         offset = sb.tile([P, 1], F32, name="offset")
         nc.vector.memset(ones[:], 1.0)
-        load_scales("e", e_scales, 0, "scales_e")
         nc.vector.tensor_single_scalar(offset[:], ones[:], OFFSET, ALU.mult)
         load_words("e", e_words, "slot_e")
         load_scales("x", x_scales, 4, "scales_x")
@@ -101,16 +102,22 @@ def tile_picked_ystarfm_pred_p_kernel(
 
         gather_scales("e", "picked_scales_e")
 
-        w_bf = sb.tile([P, 2, N, PACK], BF16, name="w_bf", align_bytes=64)
-        nc.scalar.copy(out=w_bf[:], in_=w_raw[:].rearrange("p w j n -> p w n j"))
+        w_bf = sb.tile([P, 3, N, PACK], BF16, name="w_bf", align_bytes=64)
+        w_codes = sb.tile([P, 3 * N], U32, name="w_codes", align_bytes=64)
+        w_scales = sb.tile([P, 3 * N], U8, name="w_scales", align_bytes=64)
+        for slot, source, sign in ((W2, 1, 1.0), (W2_NEG, 1, -1.0), (W1, 0, 1.0)):
+            nc.scalar.activation(
+                w_bf[:, slot, :, :], w_raw[:, source, :, :].rearrange("p j n -> p n j"), ACT.Copy, scale=sign
+            )
         load_words("d", d_words, "slot_d")
-        w_codes = sb.tile([P, 2 * N], U32, name="w_codes", align_bytes=64)
-        w_scales = sb.tile([P, 2 * N], U8, name="w_scales", align_bytes=64)
-        nc.vector.quantize_mx(
-            out=w_codes[:].bitcast(FP8X4), scales=w_scales[:], in_=w_bf[:].rearrange("p w n j -> p (w n j)")
-        )
+        for lo, hi in ((W2, W1), (W1, W1 + 1)):
+            nc.vector.quantize_mx(
+                out=w_codes[:, lo * N : hi * N].bitcast(FP8X4),
+                scales=w_scales[:, lo * N : hi * N],
+                in_=w_bf[:, lo:hi, :, :].rearrange("p w n j -> p (w n j)"),
+            )
 
-        def product(bank, weight, name, row0, lo, hi):
+        def product(bank, weight, name, row0, lo, hi, start=True, stop=True):
             cols = slice(weight * N, (weight + 1) * N)
             nc.tensor.matmul_mx(
                 out=bank,
@@ -118,75 +125,80 @@ def tile_picked_ystarfm_pred_p_kernel(
                 lhsT_scale=w_scales[:, cols],
                 rhs=picked_words[name][:, lo:hi].bitcast(FP8X4),
                 rhs_scale=picked_planes[name][row0:P, lo:hi],
-                start=True,
-                stop=True,
+                start=start,
+                stop=stop,
             )
 
-        def inverse_of_abs_plus_offset(tag, src, width):
-            mag = sb.tile([P, width], F32, name=tag + "_mag")
-            root = sb.tile([P, width], F32, name=tag + "_root")
-            inv = sb.tile([P, width], F32, name=tag + "_inv")
+        def inverse_root(tag, src):
+            mag = sb.tile([P, HALF], F32, name=tag + "_mag")
+            root = sb.tile([P, HALF], F32, name=tag + "_root")
             nc.scalar.activation(mag[:], src, ACT.Abs)
             nc.scalar.activation(root[:], mag[:], ACT.Abs_reciprocal_sqrt, bias=offset[:])
-            nc.scalar.activation(inv[:], root[:], ACT.Square)
-            return inv
+            return root
 
         gather_words("e", 0, S)
         gather_scales("x", "slot_e")
         c0_ps = ps.tile([P, S], F32, name="c0_ps", tag="bank_c0")
-        product(c0_ps[:], 1, "e", 0, 0, S)
-        c0 = sb.tile([P, S], F32, name="c0", tag="slot_c0")
+        product(c0_ps[:], W2, "e", 0, 0, S)
+        spec_ps = ps.tile([P, HALF], F32, name="spec_ps")
+        product(spec_ps[:], W2_NEG, "e", 0, 0, HALF, stop=False)
+        c0 = sb.tile([P, S], F32, name="c0")
         nc.scalar.copy(out=c0[:], in_=c0_ps[:])
 
         gain_ps = ps.tile([P, PACK, P], F32, name="gain_ps", tag="bank_c0")
         for t in range(PACK):
             nc.tensor.transpose(gain_ps[:, t, :], gain4[:, t : t + 1].to_broadcast([P, P]), ident[:])
+        gain = sb.tile([P, S], F32, name="gain")
+        nc.scalar.copy(out=gain[:].rearrange("p (n t) -> p n t", t=PACK), in_=gain_ps[:].rearrange("p t n -> p n t"))
 
         gather_words("x", 0, S)
         gather_scales("d", "slot_x")
-        f0_ps = ps.tile([P, S], F32, name="f0_ps")
-        product(f0_ps[:], 0, "x", 4, 0, S)
-        spec = sb.tile([P, S], F32, name="spec", tag="slot_scales_d")
-        nc.vector.tensor_tensor(spec[:], f0_ps[:], c0[:], ALU.subtract)
-        inv_spec = inverse_of_abs_plus_offset("spec", spec[:], S)
+        product(spec_ps[:], W1, "x", 4, 0, HALF, start=False)
+        f0_ps = ps.tile([P, HALF], F32, name="f0_ps")
+        product(f0_ps[:], W1, "x", 4, HALF, S)
+        spec = [
+            sb.tile([P, HALF], F32, name="spec0"),
+            sb.tile([P, HALF], F32, name="spec1", tag="slot_scales_d"),
+        ]
+        spec_root = [inverse_root("spec0", spec_ps[:])]
+        nc.scalar.copy(out=spec[0][:], in_=spec_ps[:])
+        nc.vector.tensor_tensor(spec[1][:], f0_ps[:], c0[:, HALF:S], ALU.subtract)
+        spec_root.append(inverse_root("spec1", spec[1][:]))
 
-        c1_ps = []
+        c1_ps, prior = [], []
         for h in range(HALVES):
             gather_words("d", h * HALF, (h + 1) * HALF)
             c1_ps.append(ps.tile([P, HALF], F32, name="c1_ps%d" % h))
-            product(c1_ps[h][:], 1, "d", 8, h * HALF, (h + 1) * HALF)
+            product(c1_ps[h][:], W2, "d", 8, h * HALF, (h + 1) * HALF)
+            prior.append(sb.tile([P, HALF], F32, name="prior%d" % h))
+            scaled = sb.tile([P, HALF], F32, name="scaled%d" % h)
+            nc.gpsimd.tensor_tensor(scaled[:], spec_root[h][:], gain[:, h * HALF : (h + 1) * HALF], ALU.mult)
+            nc.gpsimd.tensor_tensor(prior[h][:], scaled[:], spec_root[h][:], ALU.mult)
 
         inv_time, moved = [], []
         for h in range(HALVES):
             cols = slice(h * HALF, (h + 1) * HALF)
             change = sb.tile([P, HALF], F32, name="change%d" % h)
             nc.vector.tensor_tensor(change[:], c1_ps[h][:], c0[:, cols], ALU.subtract)
-            inv_time.append(inverse_of_abs_plus_offset("time%d" % h, change[:], HALF))
+            time_root = inverse_root("time%d" % h, change[:])
+            inv_time.append(sb.tile([P, HALF], F32, name="inv_time%d" % h))
+            nc.scalar.activation(inv_time[h][:], time_root[:], ACT.Square)
             moved.append(sb.tile([P, HALF], F32, name="moved%d" % h))
-            nc.vector.tensor_tensor(moved[h][:], c1_ps[h][:], spec[:, cols], ALU.add)
+            nc.vector.tensor_tensor(moved[h][:], c1_ps[h][:], spec[h][:], ALU.add)
 
-        prior = sb.tile([P, S], F32, name="prior", tag="slot_c0")
-        nc.vector.tensor_tensor(
-            prior[:].rearrange("p (n t) -> p n t", t=PACK),
-            inv_spec[:].rearrange("p (n t) -> p n t", t=PACK),
-            gain_ps[:].rearrange("p t n -> p n t"),
-            ALU.mult,
-        )
-
-        sums = sb.tile([P, 2, S // D], F32, name="sums")
+        result = sb.tile([P, S // D], F32, name="result")
         for h in range(HALVES):
-            cols = slice(h * HALF, (h + 1) * HALF)
             terms = sb.tile([P, 2, HALF], F32, name="terms%d" % h)
-            nc.vector.tensor_tensor(terms[:, 0, :], inv_time[h][:], prior[:, cols], ALU.mult)
+            nc.vector.tensor_tensor(terms[:, 0, :], inv_time[h][:], prior[h][:], ALU.mult)
             nc.vector.tensor_tensor(terms[:, 1, :], terms[:, 0, :], moved[h][:], ALU.mult)
+            sums = sb.tile([P, 2, GROUPS], F32, name="sums%d" % h)
             nc.vector.tensor_reduce(
-                sums[:, :, h * GROUPS : (h + 1) * GROUPS],
-                terms[:].rearrange("p q (v d) -> p q v d", d=D),
+                sums[:].rearrange("p q v -> p (q v)"),
+                terms[:].rearrange("p q (v d) -> p (q v) d", d=D),
                 AX.X,
                 ALU.add,
             )
-        inv_sum = sb.tile([P, S // D], F32, name="inv_sum")
-        result = sb.tile([P, S // D], F32, name="result")
-        nc.vector.reciprocal(inv_sum[:], sums[:, 0, :])
-        nc.vector.tensor_tensor(result[:], sums[:, 1, :], inv_sum[:], ALU.mult)
+            inv_sum = sb.tile([P, GROUPS], F32, name="inv_sum%d" % h)
+            nc.vector.reciprocal(inv_sum[:], sums[:, 0, :])
+            nc.vector.tensor_tensor(result[:, h * GROUPS : (h + 1) * GROUPS], sums[:, 1, :], inv_sum[:], ALU.mult)
         nc.sync.dma_start(out=out, in_=result[:])

@@ -183,22 +183,33 @@ def tile_picked_ystarfm_pred_p_kernel(
             time_root = inverse_root("time%d" % h, change[:])
             inv_time.append(sb.tile([P, HALF], F32, name="inv_time%d" % h))
             nc.scalar.activation(inv_time[h][:], time_root[:], ACT.Square)
+        for h in range(HALVES):
             moved.append(sb.tile([P, HALF], F32, name="moved%d" % h))
             nc.vector.tensor_tensor(moved[h][:], c1_ps[h][:], spec[h][:], ALU.add)
 
-        result = sb.tile([P, S // D], F32, name="result")
+        weight_sum = sb.tile([P, S // D], F32, name="weight_sum")
+        weighted_sum = sb.tile([P, S // D], F32, name="weighted_sum")
+        weighted = []
         for h in range(HALVES):
-            terms = sb.tile([P, 2, HALF], F32, name="terms%d" % h)
-            nc.vector.tensor_tensor(terms[:, 0, :], inv_time[h][:], prior[h][:], ALU.mult)
-            nc.vector.tensor_tensor(terms[:, 1, :], terms[:, 0, :], moved[h][:], ALU.mult)
-            sums = sb.tile([P, 2, GROUPS], F32, name="sums%d" % h)
+            weight = sb.tile([P, HALF], F32, name="weight%d" % h)
+            weighted.append(sb.tile([P, HALF], F32, name="weighted%d" % h))
+            nc.vector.tensor_tensor(weight[:], inv_time[h][:], prior[h][:], ALU.mult)
+            nc.gpsimd.tensor_tensor(weighted[h][:], weight[:], moved[h][:], ALU.mult)
             nc.vector.tensor_reduce(
-                sums[:].rearrange("p q v -> p (q v)"),
-                terms[:].rearrange("p q (v d) -> p (q v) d", d=D),
+                weight_sum[:, h * GROUPS : (h + 1) * GROUPS],
+                weight[:].rearrange("p (v d) -> p v d", d=D),
                 AX.X,
                 ALU.add,
             )
-            inv_sum = sb.tile([P, GROUPS], F32, name="inv_sum%d" % h)
-            nc.vector.reciprocal(inv_sum[:], sums[:, 0, :])
-            nc.vector.tensor_tensor(result[:, h * GROUPS : (h + 1) * GROUPS], sums[:, 1, :], inv_sum[:], ALU.mult)
+        inv_sum = sb.tile([P, S // D], F32, name="inv_sum")
+        nc.vector.reciprocal(inv_sum[:], weight_sum[:])
+        for h in range(HALVES):
+            nc.vector.tensor_reduce(
+                weighted_sum[:, h * GROUPS : (h + 1) * GROUPS],
+                weighted[h][:].rearrange("p (v d) -> p v d", d=D),
+                AX.X,
+                ALU.add,
+            )
+        result = sb.tile([P, S // D], F32, name="result")
+        nc.vector.tensor_tensor(result[:], weighted_sum[:], inv_sum[:], ALU.mult)
         nc.sync.dma_start(out=out, in_=result[:])

from contextlib import ExitStack

import concourse.mybir as mybir
from concourse.masks import make_identity

K, T, S, D, N = 512, 2048, 512, 8, 128
P = 128
PACK = 4
HALVES = 2
HALF = S // HALVES
GROUPS = HALF // D
OFFSET = 0.3
W2, W2_NEG, W1 = 0, 1, 2
FLOPS = 3 * 2 * K * N * S

F32 = mybir.dt.float32
BF16 = mybir.dt.bfloat16
I32 = mybir.dt.int32
U32 = mybir.dt.uint32
U16 = mybir.dt.uint16
U8 = mybir.dt.uint8
FP8X4 = mybir.dt.float8_e4m3fn_x4
ALU = mybir.AluOpType
ACT = mybir.ActivationFunctionType
AX = mybir.AxisListType


def tile_picked_ystarfm_pred_p_kernel(
    tc, x_words, x_scales, e_words, e_scales, d_words, d_scales, w1, w2, dist, use, offs, out
):
    nc = tc.nc
    with ExitStack() as ctx:
        sb = ctx.enter_context(tc.tile_pool(name="sb", bufs=1))
        ps = ctx.enter_context(tc.psum_pool(name="ps", bufs=1))

        offsets = sb.tile([P, S // 16], U16, name="offsets")
        nc.sync.dma_start(offsets[:], offs)

        w_raw = sb.tile([P, 2, PACK, N], F32, name="w_raw", tag="slot_d", align_bytes=64)
        nc.scalar.dma_start(out=w_raw[:, 1, :, :], in_=w2.rearrange("(p j) n -> p j n", j=PACK))
        nc.scalar.dma_start(out=w_raw[:, 0, :, :], in_=w1.rearrange("(p j) n -> p j n", j=PACK))

        tables = (("e", e_words, e_scales, 0), ("x", x_words, x_scales, 4), ("d", d_words, d_scales, 8))
        words, planes = {}, {}

        def load_scales(name, s_hbm, row0, tag):
            planes[name] = sb.tile([P, T], U8, name=name + "_scales_sb", tag=tag)
            nc.vector.memset(planes[name][:].bitcast(I32), 0)
            for q in range(4):
                nc.sync.dma_start(
                    out=planes[name][32 * q + row0 : 32 * q + row0 + 4, :].bitcast(I32),
                    in_=s_hbm[0, 4 * q : 4 * q + 4, :].bitcast(I32),
                )

        def load_words(name, w_hbm, tag):
            words[name] = sb.tile([P, T], U32, name=name + "_words_sb", tag=tag, align_bytes=64)
            nc.sync.dma_start(
                out=words[name][:].bitcast(I32),
                in_=w_hbm[0].rearrange("p n t -> p (n t)").bitcast(I32),
            )

        dist4 = sb.tile([P, PACK], F32, name="dist4")
        use4 = sb.tile([P, PACK], F32, name="use4")
        nc.gpsimd.dma_start(out=dist4[:], in_=dist[0].rearrange("(p t) -> p t", t=PACK))
        nc.gpsimd.dma_start(out=use4[:], in_=use[0].rearrange("(p t) -> p t", t=PACK))
        ident = sb.tile([P, P], F32, name="ident")
        make_identity(nc, ident[:])

        minus_one = sb.tile([P, PACK], F32, name="minus_one")
        inv_dist4 = sb.tile([P, PACK], F32, name="inv_dist4")
        gain4 = sb.tile([P, PACK], F32, name="gain4")
        nc.gpsimd.memset(minus_one[:], -1.0)
        nc.gpsimd.tensor_tensor(inv_dist4[:], dist4[:], minus_one[:], ALU.pow)
        nc.gpsimd.tensor_tensor(gain4[:], inv_dist4[:], use4[:], ALU.mult)

        load_scales("e", e_scales, 0, "scales_e")
        warm_in = sb.tile([P, 1], F32, name="warm_in", tag="slot_x", align_bytes=64)
        warm_out = sb.tile([P, 1], F32, name="warm_out", tag="slot_scales_d")
        nc.vector.memset(warm_in[:], 1.0)
        nc.scalar.activation(warm_out[:], warm_in[:], ACT.Abs_reciprocal_sqrt)
        ones = sb.tile([P, 1], F32, name="ones", tag="slot_e", align_bytes=64)
        offset = sb.tile([P, 1], F32, name="offset")
        nc.vector.memset(ones[:], 1.0)
        nc.vector.tensor_single_scalar(offset[:], ones[:], OFFSET, ALU.mult)
        load_words("e", e_words, "slot_e")
        load_scales("x", x_scales, 4, "scales_x")
        load_words("x", x_words, "slot_x")
        load_scales("d", d_scales, 8, "slot_scales_d")

        picked_words, picked_planes = {}, {}
        for name, w_hbm, s_hbm, row0 in tables:
            picked_words[name] = sb.tile([P, S], U32, name=name + "_picked_words", align_bytes=64)

        def gather_scales(name, tag):
            picked_planes[name] = sb.tile([P, S], U8, name=name + "_picked_scales", tag=tag, align_bytes=64)
            nc.vector.tensor_copy(picked_planes[name][:], planes[name][:].indirect(offsets[:]))

        def gather_words(name, lo, hi):
            nc.vector.tensor_copy(
                picked_words[name][:, lo:hi], words[name][:].indirect(offsets[:, lo // 16 : hi // 16])
            )

        gather_scales("e", "picked_scales_e")

        w_bf = sb.tile([P, 3, N, PACK], BF16, name="w_bf", align_bytes=64)
        w_codes = sb.tile([P, 3 * N], U32, name="w_codes", align_bytes=64)
        w_scales = sb.tile([P, 3 * N], U8, name="w_scales", align_bytes=64)
        for slot, source, sign in ((W2, 1, 1.0), (W2_NEG, 1, -1.0), (W1, 0, 1.0)):
            nc.scalar.activation(
                w_bf[:, slot, :, :], w_raw[:, source, :, :].rearrange("p j n -> p n j"), ACT.Copy, scale=sign
            )
        load_words("d", d_words, "slot_d")
        for lo, hi in ((W2, W1), (W1, W1 + 1)):
            nc.vector.quantize_mx(
                out=w_codes[:, lo * N : hi * N].bitcast(FP8X4),
                scales=w_scales[:, lo * N : hi * N],
                in_=w_bf[:, lo:hi, :, :].rearrange("p w n j -> p (w n j)"),
            )

        def product(bank, weight, name, row0, lo, hi, start=True, stop=True):
            cols = slice(weight * N, (weight + 1) * N)
            nc.tensor.matmul_mx(
                out=bank,
                lhsT=w_codes[:, cols].bitcast(FP8X4),
                lhsT_scale=w_scales[:, cols],
                rhs=picked_words[name][:, lo:hi].bitcast(FP8X4),
                rhs_scale=picked_planes[name][row0:P, lo:hi],
                start=start,
                stop=stop,
            )

        def inverse_root(tag, src):
            mag = sb.tile([P, HALF], F32, name=tag + "_mag")
            root = sb.tile([P, HALF], F32, name=tag + "_root")
            nc.scalar.activation(mag[:], src, ACT.Abs)
            nc.scalar.activation(root[:], mag[:], ACT.Abs_reciprocal_sqrt, bias=offset[:])
            return root

        gather_words("e", 0, S)
        gather_scales("x", "slot_e")
        c0_ps = ps.tile([P, S], F32, name="c0_ps", tag="bank_c0")
        product(c0_ps[:], W2, "e", 0, 0, S)
        spec_ps = ps.tile([P, HALF], F32, name="spec_ps")
        product(spec_ps[:], W2_NEG, "e", 0, 0, HALF, stop=False)
        c0 = sb.tile([P, S], F32, name="c0")
        nc.scalar.copy(out=c0[:], in_=c0_ps[:])

        gain_ps = ps.tile([P, PACK, P], F32, name="gain_ps", tag="bank_c0")
        for t in range(PACK):
            nc.tensor.transpose(gain_ps[:, t, :], gain4[:, t : t + 1].to_broadcast([P, P]), ident[:])
        gain = sb.tile([P, S], F32, name="gain")
        nc.scalar.copy(out=gain[:].rearrange("p (n t) -> p n t", t=PACK), in_=gain_ps[:].rearrange("p t n -> p n t"))

        gather_words("x", 0, S)
        gather_scales("d", "slot_x")
        product(spec_ps[:], W1, "x", 4, 0, HALF, start=False)
        f0_ps = ps.tile([P, HALF], F32, name="f0_ps")
        product(f0_ps[:], W1, "x", 4, HALF, S)
        spec = [
            sb.tile([P, HALF], F32, name="spec0"),
            sb.tile([P, HALF], F32, name="spec1", tag="slot_scales_d"),
        ]
        spec_root = [inverse_root("spec0", spec_ps[:])]
        nc.scalar.copy(out=spec[0][:], in_=spec_ps[:])
        nc.vector.tensor_tensor(spec[1][:], f0_ps[:], c0[:, HALF:S], ALU.subtract)
        spec_root.append(inverse_root("spec1", spec[1][:]))

        c1_ps, prior = [], []
        for h in range(HALVES):
            gather_words("d", h * HALF, (h + 1) * HALF)
            c1_ps.append(ps.tile([P, HALF], F32, name="c1_ps%d" % h))
            product(c1_ps[h][:], W2, "d", 8, h * HALF, (h + 1) * HALF)
            prior.append(sb.tile([P, HALF], F32, name="prior%d" % h))
            scaled = sb.tile([P, HALF], F32, name="scaled%d" % h)
            nc.gpsimd.tensor_tensor(scaled[:], spec_root[h][:], gain[:, h * HALF : (h + 1) * HALF], ALU.mult)
            nc.gpsimd.tensor_tensor(prior[h][:], scaled[:], spec_root[h][:], ALU.mult)

        inv_time, moved = [], []
        for h in range(HALVES):
            cols = slice(h * HALF, (h + 1) * HALF)
            change = sb.tile([P, HALF], F32, name="change%d" % h)
            nc.vector.tensor_tensor(change[:], c1_ps[h][:], c0[:, cols], ALU.subtract)
            time_root = inverse_root("time%d" % h, change[:])
            inv_time.append(sb.tile([P, HALF], F32, name="inv_time%d" % h))
            nc.scalar.activation(inv_time[h][:], time_root[:], ACT.Square)
        for h in range(HALVES):
            moved.append(sb.tile([P, HALF], F32, name="moved%d" % h))
            nc.vector.tensor_tensor(moved[h][:], c1_ps[h][:], spec[h][:], ALU.add)

        weight_sum = sb.tile([P, S // D], F32, name="weight_sum")
        weighted_sum = sb.tile([P, S // D], F32, name="weighted_sum")
        weighted = []
        for h in range(HALVES):
            weight = sb.tile([P, HALF], F32, name="weight%d" % h)
            weighted.append(sb.tile([P, HALF], F32, name="weighted%d" % h))
            nc.vector.tensor_tensor(weight[:], inv_time[h][:], prior[h][:], ALU.mult)
            nc.gpsimd.tensor_tensor(weighted[h][:], weight[:], moved[h][:], ALU.mult)
            nc.vector.tensor_reduce(
                weight_sum[:, h * GROUPS : (h + 1) * GROUPS],
                weight[:].rearrange("p (v d) -> p v d", d=D),
                AX.X,
                ALU.add,
            )
        inv_sum = sb.tile([P, S // D], F32, name="inv_sum")
        nc.vector.reciprocal(inv_sum[:], weight_sum[:])
        for h in range(HALVES):
            nc.vector.tensor_reduce(
                weighted_sum[:, h * GROUPS : (h + 1) * GROUPS],
                weighted[h][:].rearrange("p (v d) -> p v d", d=D),
                AX.X,
                ALU.add,
            )
        result = sb.tile([P, S // D], F32, name="result")
        nc.vector.tensor_tensor(result[:], weighted_sum[:], inv_sum[:], ALU.mult)
        nc.sync.dma_start(out=out, in_=result[:])
